import numpy as np
import ml_dtypes


def mxq(x, axis, fmt="e4m3"):
    dtype, down = {"e4m3": (ml_dtypes.float8_e4m3fn, 7), "e5m2": (ml_dtypes.float8_e5m2, 14)}[fmt]
    v = np.moveaxis(np.asarray(x, np.float32).astype(ml_dtypes.bfloat16).astype(np.float64), axis, -1)
    blocks = v.reshape(v.shape[:-1] + (-1, 32))
    amax = np.abs(blocks).max(-1, keepdims=True)
    byte = np.maximum(np.where(amax > 0, np.frexp(amax)[1] - 1 + 127, 0) - down, 1)
    scale = np.exp2(byte - 127.0)
    codes = (blocks / scale).astype(np.float32).astype(dtype).astype(np.float64)
    return np.moveaxis((codes * scale).reshape(v.shape), -1, axis)


WIDE = False


def mx_kscale(k):
    if not WIDE:
        return np.ones(k)
    levels = np.array([10, -10, 5, -5, 0])
    if k % 512:
        return np.exp2(np.random.permutation(np.resize(levels, k // 32))).repeat(32)
    a = np.empty((k // 512, 16))
    for p in range(k // 512):
        a[p, :8] = np.random.permutation(np.resize(levels, 8))
        for g in range(8):
            far = levels[np.abs(levels - a[p, g]) >= 10]
            a[p, g + 8] = far[np.random.randint(len(far))]
    return np.exp2(a.ravel()).repeat(32)


def f64(x):
    return np.asarray(x).astype(np.float64)


def striped(idx):
    return np.tile(idx.reshape(-1, 16).T, (8, 1)).astype(np.uint16)


def unstriped(offs):
    return offs[:16].T.reshape(-1).astype(np.int64)


E2M1 = np.array([0.0, 0.5, 1.0, 1.5, 2.0, 3.0, 4.0, 6.0, -0.0, -0.5, -1.0, -1.5, -2.0, -3.0, -4.0, -6.0])


def pack_weight(w, fmt):
    k, n = w.shape
    w = f64(np.asarray(w, np.float32).astype(ml_dtypes.bfloat16)).reshape(k // 32, 32, n)
    amax = np.abs(w).max(1)
    if fmt == "e4m3":
        byte = np.frexp(amax)[1] - 1 + 127 - 7
    else:
        mant, ex = np.frexp(amax / 6.0)
        byte = np.where(mant > 0.5, ex, ex - 1) + 127
    byte = np.clip(np.where(amax > 0, byte, 1), 1, 254)
    scaled = (w * np.exp2(127.0 - byte)[:, None, :]).reshape(k, n).astype(np.float32)
    by_word = np.ascontiguousarray(scaled.reshape(k // 512, 128, 4, n).transpose(0, 1, 3, 2))
    if fmt == "e4m3":
        words = by_word.astype(ml_dtypes.float8_e4m3fn).view(np.uint8)
    else:
        c = by_word.astype(ml_dtypes.float4_e2m1fn).view(np.uint8) & 0xF
        words = (c[..., 0::2] | (c[..., 1::2] << 4)).reshape(k // 512, 128, 2 * n)
    return np.ascontiguousarray(words), np.ascontiguousarray(byte.astype(np.uint8).reshape(k // 512, 16, n))


def unpack_weight(words, scales, fmt):
    g, _, n = scales.shape
    words = np.ascontiguousarray(words).reshape(g, 128, n, -1)
    if fmt == "e4m3":
        vals = words.view(ml_dtypes.float8_e4m3fn).astype(np.float64)
    else:
        nib = np.empty((g, 128, n, 4), np.uint8)
        nib[..., 0::2] = words & 0xF
        nib[..., 1::2] = words >> 4
        vals = E2M1[nib]
    vals = vals * np.repeat(np.exp2(scales.astype(np.float64) - 127.0), 8, axis=1)[..., None]
    return vals.transpose(0, 1, 3, 2).reshape(g * 512, n)


def gelu(v):
    return 0.5 * v * (1.0 + np.tanh(np.sqrt(2.0 / np.pi) * (v + 0.044715 * v**3)))


def striped8(idx):
    return np.concatenate([v.reshape(-1, 16).T for v in idx]).astype(np.uint16)


def unstriped8(offs):
    return np.stack([offs[16 * g:16 * g + 16].T.reshape(-1) for g in range(8)]).astype(np.int64)


def runs(v, idx8):
    k = np.arange(v.shape[0])
    return v[k[:, None], idx8[k % 512 // 64]]


def often(T, S):
    return np.random.permutation(T)[(T * np.random.uniform(0, 1, S) ** 4).astype(np.int64)]


K, T, S, H, P, N = 1536, 2048, 1024, 1024, 512, 768


def setup_inputs():
    n = np.random.standard_normal
    s = mx_kscale(K)[:, None]
    u = mx_kscale(H)[:, None]
    d = {}
    d["tab_words"], d["tab_scales"] = pack_weight(n((K, T)) * s, "e4m3")
    d["offs"] = striped8(np.stack([often(T, S) for _ in range(8)]))
    d["w1_words"], d["w1_scales"] = pack_weight(n((K, H)) / s * u.T / K ** 0.5, "e2m1")
    d["skew"] = np.random.uniform(-0.8, 0.8, H).astype(np.float32)
    d["pos1"] = striped(np.random.permutation(S)[:P])
    d["pos2"] = striped(np.random.permutation(S)[:P])
    d["w2"] = (n((H, N)) / u / H ** 0.5).astype(np.float32)
    d["slope"] = n((N, P)).astype(np.float32)
    return d


def reference(tab_words, tab_scales, offs, w1_words, w1_scales, skew, pos1, pos2, w2, slope):
    v = runs(unpack_weight(tab_words, tab_scales, "e4m3"), unstriped8(offs))
    w1 = unpack_weight(w1_words, w1_scales, "e2m1")
    e = w1.T @ v
    h = e - np.abs(e) * f64(skew)[:, None]
    x = h[:, unstriped(pos1)] + np.abs(h[:, unstriped(pos2)])
    y = mxq(f64(w2), 0, "e4m3").T @ mxq(x, 0, "e4m3")
    return y * f64(slope)

@@ -1,0 +1,328 @@
+from contextlib import ExitStack
+
+import concourse.mybir as mybir
+from concourse.masks import make_identity
+
+K, T, S, H, M, N = 1536, 2048, 1024, 1024, 512, 768
+FLOPS = 2 * K * H * S + 2 * H * N * M
+
+F32 = mybir.dt.float32
+BF16 = mybir.dt.bfloat16
+I32 = mybir.dt.int32
+U32 = mybir.dt.uint32
+U16 = mybir.dt.uint16
+U8 = mybir.dt.uint8
+FP8X4 = mybir.dt.float8_e4m3fn_x4
+FP4X4 = mybir.dt.float4_e2m1fn_x4
+ALU = mybir.AluOpType
+ACT = mybir.ActivationFunctionType
+
+P = 128
+PACK = 4
+PASSES1 = K // 512
+PASSES2 = H // 512
+TILES = H // P
+BANK = 512
+HALF = M // 2
+W2_PIECE = 256
+
+
+def tile_list_lane_tap_corrections_kernel(
+    tc, tab_words, tab_scales, offs, w1_words, w1_scales, skew, pos1, pos2, w2, slope, out
+):
+    nc = tc.nc
+    with ExitStack() as ctx:
+        lists = ctx.enter_context(tc.tile_pool(name="lists", bufs=1))
+        keep = ctx.enter_context(tc.tile_pool(name="keep", bufs=1))
+        ring = ctx.enter_context(tc.tile_pool(name="ring", bufs=2))
+        psum = ctx.enter_context(tc.psum_pool(name="psum", bufs=1))
+
+        def bank(j):
+            return psum.tile([P, BANK], F32, name="bank%d" % (j % 8), tag="bank%d" % (j % 8))
+
+        scale_win = ring.tile([P, T], U8, name="scale_win", tag="win", align_bytes=64)
+        nc.gpsimd.memset(scale_win[:].bitcast(I32), 0)
+        offs_t = lists.tile([P, S // 16], U16, name="offs_t")
+        nc.sync.dma_start(offs_t[:], offs)
+        for a in range(PASSES1):
+            nc.scalar.dma_start(scale_win[a:P:8, :].bitcast(I32), tab_scales[a].bitcast(I32))
+
+        def load_words(a):
+            win = ring.tile([P, T], I32, name="words_win", tag="win", align_bytes=64)
+            nc.sync.dma_start(win[:], tab_words[a].rearrange("p t i -> p (t i)").bitcast(I32))
+            return win
+
+        wins = [load_words(0)]
+
+        w1_raw = keep.tile([P, PASSES1 * 512], I32, name="w1_raw", tag="weights", align_bytes=64)
+        nc.sync.dma_start(
+            w1_raw[:].rearrange("p (a c) -> p a c", a=PASSES1),
+            w1_words.bitcast(I32).rearrange("a p c -> p a c"),
+        )
+        pos1_t = lists.tile([P, M // 16], U16, name="pos1_t")
+        nc.sync.dma_start(pos1_t[:], pos1)
+        pos2_t = lists.tile([P, M // 16], U16, name="pos2_t")
+        nc.sync.dma_start(pos2_t[:], pos2)
+
+        w1s_raw = keep.tile([P, PASSES1 * 256], I32, name="w1s_raw", align_bytes=64)
+        nc.vector.memset(w1s_raw[:], 0)
+        for d in range(4):
+            nc.gpsimd.dma_start(
+                w1s_raw[32 * d : 32 * d + 4, :].rearrange("p (a c) -> p a c", a=PASSES1),
+                w1_scales[:, 4 * d : 4 * d + 4, :].bitcast(I32).rearrange("a r c -> r a c"),
+            )
+        skew_rows = keep.tile([P, PASSES2 * P], F32, name="skew_rows")
+        nc.vector.memset(skew_rows[:], 0.0)
+        nc.gpsimd.dma_start(
+            skew_rows[0:PACK, :].rearrange("t (c l) -> t c l", l=4),
+            skew.rearrange("(c t l) -> t c l", t=PACK, l=4),
+        )
+        ident = keep.tile([P, P], F32, name="ident")
+        make_identity(nc, ident[:])
+        skew_bank = bank(7)
+        for b in range(PASSES2):
+            nc.tensor.transpose(skew_bank[:, b * P : (b + 1) * P], skew_rows[:, b * P : (b + 1) * P], ident[:])
+        neg_skew = keep.tile([P, TILES], F32, name="neg_skew")
+        nc.scalar.activation(
+            neg_skew[:].rearrange("p (b t) -> p b t", t=PACK),
+            skew_bank[:, 0 : PASSES2 * P].rearrange("p (b k) -> p b k", b=PASSES2)[:, :, 0:PACK],
+            ACT.Copy,
+            scale=-1.0,
+        )
+
+        v_planes = []
+        for a in range(PASSES1):
+            plane = keep.tile([P, S], U8, name="v_plane%d" % a, align_bytes=64)
+            nc.vector.memset(plane[:].bitcast(I32), 0)
+            v_planes.append(plane)
+
+        scale_got = keep.tile([P, S], U8, name="scale_got", align_bytes=64)
+        nc.vector.tensor_copy(scale_got[:], scale_win[:].indirect(offs_t[:]))
+        for a in range(PASSES1):
+            for d in range(4):
+                nc.scalar.dma_start(
+                    v_planes[a][32 * d : 32 * d + 4, :].bitcast(I32),
+                    scale_got[32 * d + a : 32 * d + 32 : 8, :].bitcast(I32),
+                )
+
+        v_words = {}
+
+        def gather_words(a, hf):
+            got = keep.tile([P, BANK], U32, name="v_words%d_%d" % (a, hf), align_bytes=64)
+            cols = slice(hf * BANK // 16, (hf + 1) * BANK // 16)
+            nc.vector.tensor_copy(got[:], wins[a][:].bitcast(U32).indirect(offs_t[:, cols]))
+            v_words[a, hf] = got
+
+        wins.append(load_words(1))
+        gather_words(0, 0)
+        gather_words(0, 1)
+        wins.append(load_words(2))
+
+        w1_codes = keep.tile([P, PASSES1 * 512], I32, name="w1_codes", align_bytes=64)
+        nc.vector.tensor_copy(
+            w1_codes[:].rearrange("p (g t w l) -> p g t w l", t=PACK, w=32, l=2),
+            w1_raw[:].rearrange("p (g w t l) -> p g t w l", t=PACK, w=32, l=2),
+        )
+        w1_plane = keep.tile([P, PASSES1 * 256], I32, name="w1_plane", align_bytes=64)
+        nc.vector.tensor_copy(
+            w1_plane[:].rearrange("p (g t w i) -> p g w t i", t=PACK, w=8, i=4),
+            w1s_raw[:].rearrange("p (g w i t) -> p g w t i", t=PACK, w=8, i=4),
+        )
+        gather_words(1, 0)
+        gather_words(1, 1)
+        gather_words(2, 0)
+        gather_words(2, 1)
+
+        w2_raw = []
+        for b in range(PASSES2):
+            if b == 0:
+                raw = keep.tile([P, PACK * N], F32, name="w2_raw0", tag="weights", align_bytes=64)
+            else:
+                raw = ring.tile([P, PACK * N], F32, name="w2_raw1", tag="win", align_bytes=64)
+            for l in range(4):
+                nc.sync.dma_start(
+                    raw[l:P:4, :].rearrange("w (t n) -> w t n", t=PACK),
+                    w2.rearrange("(b w t l) n -> b l w t n", b=PASSES2, t=PACK, l=4)[b, l],
+                )
+            w2_raw.append(raw)
+        slope_t = ring.tile([P, N // P, M], F32, name="slope_t", tag="win", align_bytes=64)
+        nc.sync.dma_start(slope_t[:], slope.rearrange("(c p) m -> p c m", p=P))
+
+        w2_codes = [keep.tile([P, N], U32, name="w2_codes%d" % b, align_bytes=64) for b in range(PASSES2)]
+        w2_plane = [keep.tile([P, N], U8, name="w2_plane%d" % b, align_bytes=64) for b in range(PASSES2)]
+        w2_round = {}
+
+        def round_w2(piece):
+            b, j = divmod(piece, N // W2_PIECE)
+            rounded = ring.tile([P, W2_PIECE * PACK], BF16, name="w2_round", align_bytes=64, bufs=3)
+            src = w2_raw[b][:].rearrange("p (t n) -> p t n", t=PACK)[:, :, j * W2_PIECE : (j + 1) * W2_PIECE]
+            nc.scalar.copy(
+                rounded[:].rearrange("p (c i t) -> p c t i", i=4, t=PACK),
+                src.rearrange("p t (c i) -> p c t i", i=4),
+            )
+            w2_round[piece] = rounded
+
+        def quantize_w2(piece):
+            b, j = divmod(piece, N // W2_PIECE)
+            cols = slice(j * W2_PIECE, (j + 1) * W2_PIECE)
+            nc.vector.quantize_mx(w2_codes[b][:, cols].bitcast(FP8X4), w2_plane[b][:, cols], w2_round[piece][:])
+
+        e_banks = {}
+
+        def first_pass(i, hf, a):
+            if a == 0:
+                e_banks[i, hf] = bank(2 * i + hf)
+            codes = w1_codes[:, 512 * a + 64 * i : 512 * a + 64 * (i + 1)]
+            scales = w1_plane[:, 256 * a + 32 * i : 256 * a + 32 * (i + 1)]
+            nc.tensor.matmul_mx(
+                e_banks[i, hf][:],
+                lhsT=codes.bitcast(FP4X4),
+                lhsT_scale=scales.bitcast(U8),
+                rhs=v_words[a, hf][:].bitcast(FP8X4),
+                rhs_scale=v_planes[a][:, hf * BANK : (hf + 1) * BANK],
+                start=(a == 0),
+                stop=(a == PASSES1 - 1),
+            )
+
+        for a in range(PASSES1):
+            for hf in range(2):
+                for i in range(2):
+                    first_pass(i, hf, a)
+        for i in range(2, TILES // 2):
+            for hf in range(2):
+                for a in range(PASSES1):
+                    first_pass(i, hf, a)
+
+        e_abs = {}
+
+        def magnitude(i, hf):
+            mag = ring.tile([P, BANK], F32, name="e_abs", bufs=6)
+            nc.scalar.activation(mag[:], e_banks[i, hf][:], ACT.Abs)
+            e_abs[i, hf] = mag
+
+        h_tiles = [keep.tile([P, S], F32, name="h%d" % i, align_bytes=64) for i in range(TILES)]
+        after = [keep.tile([P, M], F32, name="after%d" % i, align_bytes=64) for i in range(TILES)]
+        x_f32 = {
+            (b, part): keep.tile([P, PACK, HALF], F32, name="x%d_%d" % (b, part), align_bytes=64)
+            for b in range(PASSES2)
+            for part in range(2)
+        }
+        x_round, x_codes, x_plane = {}, {}, {}
+
+        def features(i, hf):
+            nc.vector.scalar_tensor_tensor(
+                h_tiles[i][:, hf * BANK : (hf + 1) * BANK],
+                e_abs[i, hf][:],
+                neg_skew[:, i : i + 1],
+                e_banks[i, hf][:],
+                ALU.mult,
+                ALU.add,
+            )
+
+        def pick_after(i):
+            picked = ring.tile([P, M], F32, name="picked", bufs=3)
+            nc.vector.tensor_copy(picked[:], h_tiles[i][:].indirect(pos2_t[:]))
+            nc.scalar.activation(after[i][:], picked[:], ACT.Abs)
+
+        def pick_before(i, part):
+            b, t = divmod(i, PACK)
+            cols = slice(part * HALF // 16, (part + 1) * HALF // 16)
+            nc.vector.tensor_tensor(
+                x_f32[b, part][:, t, :],
+                h_tiles[i][:].indirect(pos1_t[:, cols]),
+                after[i][:, part * HALF : (part + 1) * HALF],
+                ALU.add,
+            )
+
+        def round_x(b, part):
+            rounded = keep.tile([P, HALF * PACK], BF16, name="x_round%d_%d" % (b, part), align_bytes=64)
+            nc.scalar.copy(
+                rounded[:].rearrange("p (c i t) -> p c t i", i=4, t=PACK),
+                x_f32[b, part][:].rearrange("p t (c i) -> p c t i", i=4),
+            )
+            x_round[b, part] = rounded
+
+        def quantize_x(b, part):
+            codes = keep.tile([P, HALF], U32, name="x_codes%d_%d" % (b, part), align_bytes=64)
+            plane = keep.tile([P, HALF], U8, name="x_plane%d_%d" % (b, part), align_bytes=64)
+            nc.vector.quantize_mx(codes[:].bitcast(FP8X4), plane[:], x_round[b, part][:])
+            x_codes[b, part], x_plane[b, part] = codes, plane
+
+        y_banks = {}
+
+        def second_product(part):
+            for pair in range(N // P // 2):
+                acc = bank(3 * part + pair)
+                for u in range(2):
+                    c = 2 * pair + u
+                    for b in range(PASSES2):
+                        nc.tensor.matmul_mx(
+                            acc[:, u * HALF : (u + 1) * HALF],
+                            lhsT=w2_codes[b][:, c * P : (c + 1) * P].bitcast(FP8X4),
+                            lhsT_scale=w2_plane[b][:, c * P : (c + 1) * P],
+                            rhs=x_codes[b, part][:].bitcast(FP8X4),
+                            rhs_scale=x_plane[b, part][:],
+                            start=(b == 0),
+                            stop=(b == PASSES2 - 1),
+                        )
+                y_banks[part, pair] = acc
+
+        def finish(part, pair):
+            cols = slice(part * HALF, (part + 1) * HALF)
+            res = ring.tile([P, 2, HALF], F32, name="res", bufs=6)
+            nc.vector.tensor_tensor(
+                res[:],
+                y_banks[part, pair][:].rearrange("p (u m) -> p u m", u=2),
+                slope_t[:, 2 * pair : 2 * pair + 2, cols],
+                ALU.mult,
+            )
+            nc.sync.dma_start(out.rearrange("(c p) m -> p c m", p=P)[:, 2 * pair : 2 * pair + 2, cols], res[:])
+
+        for hf in range(2):
+            for i in range(2):
+                magnitude(i, hf)
+        features(0, 0)
+        features(1, 0)
+        features(0, 1)
+        for i in range(TILES):
+            if i + 2 < TILES:
+                magnitude(i + 2, 0)
+                magnitude(i + 2, 1)
+            if i + TILES // 2 < TILES:
+                for hf in range(2):
+                    for a in range(PASSES1):
+                        first_pass(i + TILES // 2, hf, a)
+            pick_after(i)
+            if i >= 2:
+                round_w2(i - 2)
+            if i + 1 < TILES:
+                if i >= 1:
+                    features(i + 1, 0)
+                features(i + 1, 1)
+            if i >= 3:
+                quantize_w2(i - 3)
+            if i < TILES - 1:
+                pick_before(i, 0)
+            if i == PACK - 1:
+                round_x(0, 0)
+            if i == PACK:
+                quantize_x(0, 0)
+        quantize_w2(5)
+        pick_before(TILES - 1, 0)
+        round_x(1, 0)
+        for i in range(PACK):
+            pick_before(i, 1)
+        quantize_x(1, 0)
+        round_x(0, 1)
+        second_product(0)
+        for i in range(PACK, TILES):
+            pick_before(i, 1)
+        round_x(1, 1)
+        quantize_x(0, 1)
+        finish(0, 0)
+        finish(0, 1)
+        quantize_x(1, 1)
+        second_product(1)
+        finish(0, 2)
+        for pair in range(3):
+            finish(1, pair)

@@ -40,29 +40,29 @@ def tile_list_lane_tap_corrections_kernel(
         def bank(j):
             return psum.tile([P, BANK], F32, name="bank%d" % (j % 8), tag="bank%d" % (j % 8))
 
-        scale_win = ring.tile([P, T], U8, name="scale_win", tag="win", align_bytes=64)
+        scale_win = keep.tile([P, T], U8, name="scale_win", tag="slot_a", align_bytes=64)
         nc.gpsimd.memset(scale_win[:].bitcast(I32), 0)
         offs_t = lists.tile([P, S // 16], U16, name="offs_t")
         nc.sync.dma_start(offs_t[:], offs)
+        pos2_t = lists.tile([P, M // 16], U16, name="pos2_t")
+        nc.sync.dma_start(pos2_t[:], pos2)
+        pos1_t = lists.tile([P, M // 16], U16, name="pos1_t")
+        nc.sync.dma_start(pos1_t[:], pos1)
         for a in range(PASSES1):
-            nc.scalar.dma_start(scale_win[a:P:8, :].bitcast(I32), tab_scales[a].bitcast(I32))
+            nc.sync.dma_start(scale_win[a:P:8, :].bitcast(I32), tab_scales[a].bitcast(I32))
 
-        def load_words(a):
-            win = ring.tile([P, T], I32, name="words_win", tag="win", align_bytes=64)
+        def load_words(a, slot):
+            win = keep.tile([P, T], I32, name="words_win%d" % a, tag=slot, align_bytes=64)
             nc.sync.dma_start(win[:], tab_words[a].rearrange("p t i -> p (t i)").bitcast(I32))
             return win
 
-        wins = [load_words(0)]
-
-        w1_raw = keep.tile([P, PASSES1 * 512], I32, name="w1_raw", tag="weights", align_bytes=64)
+        wins = [load_words(0, "slot_b")]
+        w1_raw = keep.tile([P, PASSES1 * 512], I32, name="w1_raw", tag="slot_d", align_bytes=64)
         nc.sync.dma_start(
             w1_raw[:].rearrange("p (a c) -> p a c", a=PASSES1),
             w1_words.bitcast(I32).rearrange("a p c -> p a c"),
         )
-        pos1_t = lists.tile([P, M // 16], U16, name="pos1_t")
-        nc.sync.dma_start(pos1_t[:], pos1)
-        pos2_t = lists.tile([P, M // 16], U16, name="pos2_t")
-        nc.sync.dma_start(pos2_t[:], pos2)
+        wins.append(load_words(1, "slot_c"))
 
         w1s_raw = keep.tile([P, PASSES1 * 256], I32, name="w1s_raw", align_bytes=64)
         nc.vector.memset(w1s_raw[:], 0)
@@ -100,10 +100,12 @@ def tile_list_lane_tap_corrections_kernel(
         nc.vector.tensor_copy(scale_got[:], scale_win[:].indirect(offs_t[:]))
         for a in range(PASSES1):
             for d in range(4):
-                nc.scalar.dma_start(
+                nc.sync.dma_start(
                     v_planes[a][32 * d : 32 * d + 4, :].bitcast(I32),
                     scale_got[32 * d + a : 32 * d + 32 : 8, :].bitcast(I32),
                 )
+                if (a, d) == (1, 0):
+                    wins.append(load_words(2, "slot_a"))
 
         v_words = {}
 
@@ -113,10 +115,8 @@ def tile_list_lane_tap_corrections_kernel(
             nc.vector.tensor_copy(got[:], wins[a][:].bitcast(U32).indirect(offs_t[:, cols]))
             v_words[a, hf] = got
 
-        wins.append(load_words(1))
         gather_words(0, 0)
         gather_words(0, 1)
-        wins.append(load_words(2))
 
         w1_codes = keep.tile([P, PASSES1 * 512], I32, name="w1_codes", align_bytes=64)
         nc.vector.tensor_copy(
@@ -124,9 +124,9 @@ def tile_list_lane_tap_corrections_kernel(
             w1_raw[:].rearrange("p (g w t l) -> p g t w l", t=PACK, w=32, l=2),
         )
         w1_plane = keep.tile([P, PASSES1 * 256], I32, name="w1_plane", align_bytes=64)
-        nc.vector.tensor_copy(
-            w1_plane[:].rearrange("p (g t w i) -> p g w t i", t=PACK, w=8, i=4),
-            w1s_raw[:].rearrange("p (g w i t) -> p g w t i", t=PACK, w=8, i=4),
+        nc.gpsimd.tensor_copy(
+            w1_plane[:].rearrange("p (g t w) -> p g t w", t=PACK, w=32),
+            w1s_raw[:].rearrange("p (g w t) -> p g t w", t=PACK, w=32),
         )
         gather_words(1, 0)
         gather_words(1, 1)
@@ -135,17 +135,14 @@ def tile_list_lane_tap_corrections_kernel(
 
         w2_raw = []
         for b in range(PASSES2):
-            if b == 0:
-                raw = keep.tile([P, PACK * N], F32, name="w2_raw0", tag="weights", align_bytes=64)
-            else:
-                raw = ring.tile([P, PACK * N], F32, name="w2_raw1", tag="win", align_bytes=64)
+            raw = keep.tile([P, PACK * N], F32, name="w2_raw%d" % b, tag=("slot_d", "slot_c")[b], align_bytes=64)
             for l in range(4):
                 nc.sync.dma_start(
                     raw[l:P:4, :].rearrange("w (t n) -> w t n", t=PACK),
                     w2.rearrange("(b w t l) n -> b l w t n", b=PASSES2, t=PACK, l=4)[b, l],
                 )
             w2_raw.append(raw)
-        slope_t = ring.tile([P, N // P, M], F32, name="slope_t", tag="win", align_bytes=64)
+        slope_t = keep.tile([P, N // P, M], F32, name="slope_t", tag="slot_b", align_bytes=64)
         nc.sync.dma_start(slope_t[:], slope.rearrange("(c p) m -> p c m", p=P))
 
         w2_codes = [keep.tile([P, N], U32, name="w2_codes%d" % b, align_bytes=64) for b in range(PASSES2)]
@@ -171,7 +168,7 @@ def tile_list_lane_tap_corrections_kernel(
 
         def first_pass(i, hf, a):
             if a == 0:
-                e_banks[i, hf] = bank(2 * i + hf)
+                e_banks[i, hf] = bank((2 * i + hf) % 4)
             codes = w1_codes[:, 512 * a + 64 * i : 512 * a + 64 * (i + 1)]
             scales = w1_plane[:, 256 * a + 32 * i : 256 * a + 32 * (i + 1)]
             nc.tensor.matmul_mx(
@@ -188,10 +185,7 @@ def tile_list_lane_tap_corrections_kernel(
             for hf in range(2):
                 for i in range(2):
                     first_pass(i, hf, a)
-        for i in range(2, TILES // 2):
-            for hf in range(2):
-                for a in range(PASSES1):
-                    first_pass(i, hf, a)
+
 
         e_abs = {}
 
@@ -252,7 +246,7 @@ def tile_list_lane_tap_corrections_kernel(
 
         def second_product(part):
             for pair in range(N // P // 2):
-                acc = bank(3 * part + pair)
+                acc = bank(4 + 3 * part + pair)
                 for u in range(2):
                     c = 2 * pair + u
                     for b in range(PASSES2):
@@ -286,12 +280,10 @@ def tile_list_lane_tap_corrections_kernel(
         features(0, 1)
         for i in range(TILES):
             if i + 2 < TILES:
-                magnitude(i + 2, 0)
-                magnitude(i + 2, 1)
-            if i + TILES // 2 < TILES:
                 for hf in range(2):
                     for a in range(PASSES1):
-                        first_pass(i + TILES // 2, hf, a)
+                        first_pass(i + 2, hf, a)
+                    magnitude(i + 2, hf)
             pick_after(i)
             if i >= 2:
                 round_w2(i - 2)

@@ -57,6 +57,13 @@ def tile_list_lane_tap_corrections_kernel(
             return win
 
         wins = [load_words(0, "slot_b")]
+        w1s_raw = keep.tile([P, PASSES1 * 256], I32, name="w1s_raw", align_bytes=64)
+        nc.vector.memset(w1s_raw[:], 0)
+        for d in range(4):
+            nc.sync.dma_start(
+                w1s_raw[32 * d : 32 * d + 4, :].rearrange("p (a c) -> p a c", a=PASSES1),
+                w1_scales[:, 4 * d : 4 * d + 4, :].bitcast(I32).rearrange("a r c -> r a c"),
+            )
         w1_raw = keep.tile([P, PASSES1 * 512], I32, name="w1_raw", tag="slot_d", align_bytes=64)
         nc.sync.dma_start(
             w1_raw[:].rearrange("p (a c) -> p a c", a=PASSES1),
@@ -64,16 +71,9 @@ def tile_list_lane_tap_corrections_kernel(
         )
         wins.append(load_words(1, "slot_c"))
 
-        w1s_raw = keep.tile([P, PASSES1 * 256], I32, name="w1s_raw", align_bytes=64)
-        nc.vector.memset(w1s_raw[:], 0)
-        for d in range(4):
-            nc.gpsimd.dma_start(
-                w1s_raw[32 * d : 32 * d + 4, :].rearrange("p (a c) -> p a c", a=PASSES1),
-                w1_scales[:, 4 * d : 4 * d + 4, :].bitcast(I32).rearrange("a r c -> r a c"),
-            )
         skew_rows = keep.tile([P, PASSES2 * P], F32, name="skew_rows")
         nc.vector.memset(skew_rows[:], 0.0)
-        nc.gpsimd.dma_start(
+        nc.sync.dma_start(
             skew_rows[0:PACK, :].rearrange("t (c l) -> t c l", l=4),
             skew.rearrange("(c t l) -> t c l", t=PACK, l=4),
         )
@@ -109,14 +109,14 @@ def tile_list_lane_tap_corrections_kernel(
 
         v_words = {}
 
-        def gather_words(a, hf):
-            got = keep.tile([P, BANK], U32, name="v_words%d_%d" % (a, hf), align_bytes=64)
-            cols = slice(hf * BANK // 16, (hf + 1) * BANK // 16)
+        def gather_words(a, first, width):
+            got = keep.tile([P, width], U32, name="v_words%d_%d" % (a, first), align_bytes=64)
+            cols = slice(first // 16, (first + width) // 16)
             nc.vector.tensor_copy(got[:], wins[a][:].bitcast(U32).indirect(offs_t[:, cols]))
-            v_words[a, hf] = got
+            for j in range(0, width, BANK):
+                v_words[a, (first + j) // BANK] = got[:, j : j + BANK]
 
-        gather_words(0, 0)
-        gather_words(0, 1)
+        gather_words(0, 0, S)
 
         w1_codes = keep.tile([P, PASSES1 * 512], I32, name="w1_codes", align_bytes=64)
         nc.vector.tensor_copy(
@@ -124,14 +124,14 @@ def tile_list_lane_tap_corrections_kernel(
             w1_raw[:].rearrange("p (g w t l) -> p g t w l", t=PACK, w=32, l=2),
         )
         w1_plane = keep.tile([P, PASSES1 * 256], I32, name="w1_plane", align_bytes=64)
-        nc.gpsimd.tensor_copy(
-            w1_plane[:].rearrange("p (g t w) -> p g t w", t=PACK, w=32),
-            w1s_raw[:].rearrange("p (g w t) -> p g t w", t=PACK, w=32),
+        nc.vector.tensor_copy(
+            w1_plane[:].rearrange("p (g t w i) -> p g w t i", t=PACK, w=8, i=4),
+            w1s_raw[:].rearrange("p (g w i t) -> p g w t i", t=PACK, w=8, i=4),
         )
-        gather_words(1, 0)
-        gather_words(1, 1)
-        gather_words(2, 0)
-        gather_words(2, 1)
+        gather_words(1, 0, BANK)
+        gather_words(1, BANK, BANK)
+        gather_words(2, 0, BANK)
+        gather_words(2, BANK, BANK)
 
         w2_raw = []
         for b in range(PASSES2):
@@ -175,7 +175,7 @@ def tile_list_lane_tap_corrections_kernel(
                 e_banks[i, hf][:],
                 lhsT=codes.bitcast(FP4X4),
                 lhsT_scale=scales.bitcast(U8),
-                rhs=v_words[a, hf][:].bitcast(FP8X4),
+                rhs=v_words[a, hf].bitcast(FP8X4),
                 rhs_scale=v_planes[a][:, hf * BANK : (hf + 1) * BANK],
                 start=(a == 0),
                 stop=(a == PASSES1 - 1),
@@ -196,10 +196,10 @@ def tile_list_lane_tap_corrections_kernel(
 
         h_tiles = [keep.tile([P, S], F32, name="h%d" % i, align_bytes=64) for i in range(TILES)]
         after = [keep.tile([P, M], F32, name="after%d" % i, align_bytes=64) for i in range(TILES)]
+        spans = [(0, 0, M), (1, 0, HALF), (1, HALF, HALF)]
         x_f32 = {
-            (b, part): keep.tile([P, PACK, HALF], F32, name="x%d_%d" % (b, part), align_bytes=64)
-            for b in range(PASSES2)
-            for part in range(2)
+            (b, m0): keep.tile([P, PACK, width], F32, name="x%d_%d" % (b, m0), align_bytes=64)
+            for b, m0, width in spans
         }
         x_round, x_codes, x_plane = {}, {}, {}
 
@@ -218,48 +218,49 @@ def tile_list_lane_tap_corrections_kernel(
             nc.vector.tensor_copy(picked[:], h_tiles[i][:].indirect(pos2_t[:]))
             nc.scalar.activation(after[i][:], picked[:], ACT.Abs)
 
-        def pick_before(i, part):
+        def pick_before(i, m0, width):
             b, t = divmod(i, PACK)
-            cols = slice(part * HALF // 16, (part + 1) * HALF // 16)
             nc.vector.tensor_tensor(
-                x_f32[b, part][:, t, :],
-                h_tiles[i][:].indirect(pos1_t[:, cols]),
-                after[i][:, part * HALF : (part + 1) * HALF],
+                x_f32[b, m0][:, t, :],
+                h_tiles[i][:].indirect(pos1_t[:, m0 // 16 : (m0 + width) // 16]),
+                after[i][:, m0 : m0 + width],
                 ALU.add,
             )
 
-        def round_x(b, part):
-            rounded = keep.tile([P, HALF * PACK], BF16, name="x_round%d_%d" % (b, part), align_bytes=64)
-            nc.scalar.copy(
-                rounded[:].rearrange("p (c i t) -> p c t i", i=4, t=PACK),
-                x_f32[b, part][:].rearrange("p t (c i) -> p c t i", i=4),
-            )
-            x_round[b, part] = rounded
+        def round_x(b, m0, width):
+            rounded = keep.tile([P, width * PACK], BF16, name="x_round%d_%d" % (b, m0), align_bytes=64)
+            for j in range(0, width, HALF):
+                nc.scalar.copy(
+                    rounded[:, j * PACK : (j + HALF) * PACK].rearrange("p (c i t) -> p c t i", i=4, t=PACK),
+                    x_f32[b, m0][:, :, j : j + HALF].rearrange("p t (c i) -> p c t i", i=4),
+                )
+            x_round[b, m0] = rounded
 
-        def quantize_x(b, part):
-            codes = keep.tile([P, HALF], U32, name="x_codes%d_%d" % (b, part), align_bytes=64)
-            plane = keep.tile([P, HALF], U8, name="x_plane%d_%d" % (b, part), align_bytes=64)
-            nc.vector.quantize_mx(codes[:].bitcast(FP8X4), plane[:], x_round[b, part][:])
-            x_codes[b, part], x_plane[b, part] = codes, plane
+        def quantize_x(b, m0, width):
+            codes = keep.tile([P, width], U32, name="x_codes%d_%d" % (b, m0), align_bytes=64)
+            plane = keep.tile([P, width], U8, name="x_plane%d_%d" % (b, m0), align_bytes=64)
+            nc.vector.quantize_mx(codes[:].bitcast(FP8X4), plane[:], x_round[b, m0][:])
+            for j in range(0, width, HALF):
+                x_codes[b, (m0 + j) // HALF] = codes[:, j : j + HALF]
+                x_plane[b, (m0 + j) // HALF] = plane[:, j : j + HALF]
 
         y_banks = {}
 
-        def second_product(part):
+        def second_pass(b, part):
             for pair in range(N // P // 2):
-                acc = bank(4 + 3 * part + pair)
+                if b == 0:
+                    y_banks[part, pair] = bank(4 + 3 * part + pair)
                 for u in range(2):
                     c = 2 * pair + u
-                    for b in range(PASSES2):
-                        nc.tensor.matmul_mx(
-                            acc[:, u * HALF : (u + 1) * HALF],
-                            lhsT=w2_codes[b][:, c * P : (c + 1) * P].bitcast(FP8X4),
-                            lhsT_scale=w2_plane[b][:, c * P : (c + 1) * P],
-                            rhs=x_codes[b, part][:].bitcast(FP8X4),
-                            rhs_scale=x_plane[b, part][:],
-                            start=(b == 0),
-                            stop=(b == PASSES2 - 1),
-                        )
-                y_banks[part, pair] = acc
+                    nc.tensor.matmul_mx(
+                        y_banks[part, pair][:, u * HALF : (u + 1) * HALF],
+                        lhsT=w2_codes[b][:, c * P : (c + 1) * P].bitcast(FP8X4),
+                        lhsT_scale=w2_plane[b][:, c * P : (c + 1) * P],
+                        rhs=x_codes[b, part].bitcast(FP8X4),
+                        rhs_scale=x_plane[b, part],
+                        start=(b == 0 and u == 0),
+                        stop=(b == PASSES2 - 1 and u == 1),
+                    )
 
         def finish(part, pair):
             cols = slice(part * HALF, (part + 1) * HALF)
@@ -293,28 +294,25 @@ def tile_list_lane_tap_corrections_kernel(
                 features(i + 1, 1)
             if i >= 3:
                 quantize_w2(i - 3)
-            if i < TILES - 1:
-                pick_before(i, 0)
+            pick_before(i, 0, M if i < PACK else HALF)
             if i == PACK - 1:
-                round_x(0, 0)
-            if i == PACK:
-                quantize_x(0, 0)
+                round_x(0, 0, M)
+            if i == PACK + 1:
+                quantize_x(0, 0, M)
         quantize_w2(5)
-        pick_before(TILES - 1, 0)
-        round_x(1, 0)
-        for i in range(PACK):
-            pick_before(i, 1)
-        quantize_x(1, 0)
-        round_x(0, 1)
-        second_product(0)
-        for i in range(PACK, TILES):
-            pick_before(i, 1)
-        round_x(1, 1)
-        quantize_x(0, 1)
+        second_pass(0, 0)
+        second_pass(0, 1)
+        round_x(1, 0, HALF)
+        for i in range(PACK, TILES - 1):
+            pick_before(i, HALF, HALF)
+        quantize_x(1, 0, HALF)
+        second_pass(1, 0)
+        pick_before(TILES - 1, HALF, HALF)
+        round_x(1, HALF, HALF)
         finish(0, 0)
         finish(0, 1)
-        quantize_x(1, 1)
-        second_product(1)
+        quantize_x(1, HALF, HALF)
+        second_pass(1, 1)
         finish(0, 2)
         for pair in range(3):
             finish(1, pair)

@@ -1,7 +1,6 @@
 from contextlib import ExitStack
 
 import concourse.mybir as mybir
-from concourse.masks import make_identity
 
 K, T, S, H, M, N = 1536, 2048, 1024, 1024, 512, 768
 FLOPS = 2 * K * H * S + 2 * H * N * M
@@ -44,10 +43,16 @@ def tile_list_lane_tap_corrections_kernel(
         nc.gpsimd.memset(scale_win[:].bitcast(I32), 0)
         offs_t = lists.tile([P, S // 16], U16, name="offs_t")
         nc.sync.dma_start(offs_t[:], offs)
-        pos2_t = lists.tile([P, M // 16], U16, name="pos2_t")
-        nc.sync.dma_start(pos2_t[:], pos2)
-        pos1_t = lists.tile([P, M // 16], U16, name="pos1_t")
-        nc.sync.dma_start(pos1_t[:], pos1)
+        skew_t = keep.tile([P, PASSES2, 8], F32, name="skew_t")
+
+        def load_skew(l):
+            nc.sync.dma_start(
+                skew_t[l:P:2, :, 0:7],
+                skew.rearrange("(b w j) -> w b j", b=PASSES2, j=8)[:, :, l : l + 7],
+            )
+
+        load_skew(0)
+        load_skew(1)
         for a in range(PASSES1):
             nc.sync.dma_start(scale_win[a:P:8, :].bitcast(I32), tab_scales[a].bitcast(I32))
 
@@ -59,35 +64,26 @@ def tile_list_lane_tap_corrections_kernel(
         wins = [load_words(0, "slot_b")]
         w1s_raw = keep.tile([P, PASSES1 * 256], I32, name="w1s_raw", align_bytes=64)
         nc.vector.memset(w1s_raw[:], 0)
-        for d in range(4):
+        for r in range(4):
             nc.sync.dma_start(
-                w1s_raw[32 * d : 32 * d + 4, :].rearrange("p (a c) -> p a c", a=PASSES1),
-                w1_scales[:, 4 * d : 4 * d + 4, :].bitcast(I32).rearrange("a r c -> r a c"),
+                w1s_raw[r:P:32, :].rearrange("d (a c) -> d a c", a=PASSES1),
+                w1_scales[:, r:16:4, :].bitcast(I32).rearrange("a d c -> d a c"),
             )
-        w1_raw = keep.tile([P, PASSES1 * 512], I32, name="w1_raw", tag="slot_d", align_bytes=64)
-        nc.sync.dma_start(
-            w1_raw[:].rearrange("p (a c) -> p a c", a=PASSES1),
-            w1_words.bitcast(I32).rearrange("a p c -> p a c"),
-        )
+
+        def load_w1(b, slot):
+            raw = keep.tile([P, PASSES1 * 256], I32, name="w1_raw%d" % b, tag=slot, align_bytes=64)
+            nc.sync.dma_start(
+                raw[:].rearrange("p (a c) -> p a c", a=PASSES1),
+                w1_words.bitcast(I32).rearrange("a p c -> p a c")[:, :, 256 * b : 256 * (b + 1)],
+            )
+            return raw
+
+        w1_raw = [load_w1(0, "slot_d")]
         wins.append(load_words(1, "slot_c"))
 
-        skew_rows = keep.tile([P, PASSES2 * P], F32, name="skew_rows")
-        nc.vector.memset(skew_rows[:], 0.0)
-        nc.sync.dma_start(
-            skew_rows[0:PACK, :].rearrange("t (c l) -> t c l", l=4),
-            skew.rearrange("(c t l) -> t c l", t=PACK, l=4),
-        )
-        ident = keep.tile([P, P], F32, name="ident")
-        make_identity(nc, ident[:])
-        skew_bank = bank(7)
-        for b in range(PASSES2):
-            nc.tensor.transpose(skew_bank[:, b * P : (b + 1) * P], skew_rows[:, b * P : (b + 1) * P], ident[:])
         neg_skew = keep.tile([P, TILES], F32, name="neg_skew")
         nc.scalar.activation(
-            neg_skew[:].rearrange("p (b t) -> p b t", t=PACK),
-            skew_bank[:, 0 : PASSES2 * P].rearrange("p (b k) -> p b k", b=PASSES2)[:, :, 0:PACK],
-            ACT.Copy,
-            scale=-1.0,
+            neg_skew[:].rearrange("p (b t) -> p b t", t=PACK), skew_t[:, :, 0:7:2], ACT.Copy, scale=-1.0
         )
 
         v_planes = []
@@ -99,13 +95,18 @@ def tile_list_lane_tap_corrections_kernel(
         scale_got = keep.tile([P, S], U8, name="scale_got", align_bytes=64)
         nc.vector.tensor_copy(scale_got[:], scale_win[:].indirect(offs_t[:]))
         for a in range(PASSES1):
-            for d in range(4):
+            for r in range(4):
                 nc.sync.dma_start(
-                    v_planes[a][32 * d : 32 * d + 4, :].bitcast(I32),
-                    scale_got[32 * d + a : 32 * d + 32 : 8, :].bitcast(I32),
+                    v_planes[a][r:P:32, :].bitcast(I32),
+                    scale_got[8 * r + a : P : 32, :].bitcast(I32),
                 )
-                if (a, d) == (1, 0):
+                if (a, r) == (1, 1):
                     wins.append(load_words(2, "slot_a"))
+        w1_raw.append(load_w1(1, "slot_e"))
+        pos2_t = lists.tile([P, M // 16], U16, name="pos2_t")
+        nc.sync.dma_start(pos2_t[:], pos2)
+        pos1_t = lists.tile([P, M // 16], U16, name="pos1_t")
+        nc.sync.dma_start(pos1_t[:], pos1)
 
         v_words = {}
 
@@ -118,15 +119,21 @@ def tile_list_lane_tap_corrections_kernel(
 
         gather_words(0, 0, S)
 
-        w1_codes = keep.tile([P, PASSES1 * 512], I32, name="w1_codes", align_bytes=64)
-        nc.vector.tensor_copy(
-            w1_codes[:].rearrange("p (g t w l) -> p g t w l", t=PACK, w=32, l=2),
-            w1_raw[:].rearrange("p (g w t l) -> p g t w l", t=PACK, w=32, l=2),
-        )
+        w1_codes = []
+
+        def deal_w1(b):
+            codes = keep.tile([P, PASSES1 * 256], I32, name="w1_codes%d" % b, align_bytes=64)
+            nc.vector.tensor_copy(
+                codes[:].rearrange("p (a t w i) -> p w a t i", t=PACK, w=16, i=4),
+                w1_raw[b][:].rearrange("p (a w i t) -> p w a t i", t=PACK, w=16, i=4),
+            )
+            w1_codes.append(codes)
+
+        deal_w1(0)
         w1_plane = keep.tile([P, PASSES1 * 256], I32, name="w1_plane", align_bytes=64)
         nc.vector.tensor_copy(
-            w1_plane[:].rearrange("p (g t w i) -> p g w t i", t=PACK, w=8, i=4),
-            w1s_raw[:].rearrange("p (g w i t) -> p g w t i", t=PACK, w=8, i=4),
+            w1_plane[:].bitcast(U16).rearrange("p (g t w i) -> p g w t i", t=PACK, w=8, i=8),
+            w1s_raw[:].bitcast(U16).rearrange("p (g w i t) -> p g w t i", t=PACK, w=8, i=8),
         )
         gather_words(1, 0, BANK)
         gather_words(1, BANK, BANK)
@@ -136,10 +143,10 @@ def tile_list_lane_tap_corrections_kernel(
         w2_raw = []
         for b in range(PASSES2):
             raw = keep.tile([P, PACK * N], F32, name="w2_raw%d" % b, tag=("slot_d", "slot_c")[b], align_bytes=64)
-            for l in range(4):
+            for l in range(2):
                 nc.sync.dma_start(
-                    raw[l:P:4, :].rearrange("w (t n) -> w t n", t=PACK),
-                    w2.rearrange("(b w t l) n -> b l w t n", b=PASSES2, t=PACK, l=4)[b, l],
+                    raw[l:P:2, :].rearrange("w (t n) -> w t n", t=PACK),
+                    w2.rearrange("(b w t l) n -> b l w t n", b=PASSES2, t=PACK, l=2)[b, l],
                 )
             w2_raw.append(raw)
         slope_t = keep.tile([P, N // P, M], F32, name="slope_t", tag="slot_b", align_bytes=64)
@@ -169,7 +176,8 @@ def tile_list_lane_tap_corrections_kernel(
         def first_pass(i, hf, a):
             if a == 0:
                 e_banks[i, hf] = bank((2 * i + hf) % 4)
-            codes = w1_codes[:, 512 * a + 64 * i : 512 * a + 64 * (i + 1)]
+            b, t = divmod(i, PACK)
+            codes = w1_codes[b][:, 256 * a + 64 * t : 256 * a + 64 * (t + 1)]
             scales = w1_plane[:, 256 * a + 32 * i : 256 * a + 32 * (i + 1)]
             nc.tensor.matmul_mx(
                 e_banks[i, hf][:],
@@ -262,16 +270,17 @@ def tile_list_lane_tap_corrections_kernel(
                         stop=(b == PASSES2 - 1 and u == 1),
                     )
 
-        def finish(part, pair):
+        def finish(part, c0, count):
             cols = slice(part * HALF, (part + 1) * HALF)
-            res = ring.tile([P, 2, HALF], F32, name="res", bufs=6)
+            pair, u = divmod(c0, 2)
+            res = keep.tile([P, count, HALF], F32, name="res%d_%d" % (part, c0))
             nc.vector.tensor_tensor(
                 res[:],
-                y_banks[part, pair][:].rearrange("p (u m) -> p u m", u=2),
-                slope_t[:, 2 * pair : 2 * pair + 2, cols],
+                y_banks[part, pair][:].rearrange("p (u m) -> p u m", u=2)[:, u : u + count, :],
+                slope_t[:, c0 : c0 + count, cols],
                 ALU.mult,
             )
-            nc.sync.dma_start(out.rearrange("(c p) m -> p c m", p=P)[:, 2 * pair : 2 * pair + 2, cols], res[:])
+            nc.sync.dma_start(out.rearrange("(c p) m -> p c m", p=P)[:, c0 : c0 + count, cols], res[:])
 
         for hf in range(2):
             for i in range(2):
@@ -292,6 +301,8 @@ def tile_list_lane_tap_corrections_kernel(
                 if i >= 1:
                     features(i + 1, 0)
                 features(i + 1, 1)
+            if i == 1:
+                deal_w1(1)
             if i >= 3:
                 quantize_w2(i - 3)
             pick_before(i, 0, M if i < PACK else HALF)
@@ -309,10 +320,12 @@ def tile_list_lane_tap_corrections_kernel(
         second_pass(1, 0)
         pick_before(TILES - 1, HALF, HALF)
         round_x(1, HALF, HALF)
-        finish(0, 0)
-        finish(0, 1)
+        finish(0, 0, 2)
+        finish(0, 2, 2)
         quantize_x(1, HALF, HALF)
         second_pass(1, 1)
-        finish(0, 2)
-        for pair in range(3):
-            finish(1, pair)
+        finish(0, 4, 2)
+        finish(1, 0, 2)
+        finish(1, 2, 2)
+        finish(1, 4, 1)
+        finish(1, 5, 1)

@@ -18,12 +18,18 @@ ACT = mybir.ActivationFunctionType
 
 P = 128
 PACK = 4
-PASSES1 = K // 512
-PASSES2 = H // 512
+GROUP = 16
+K_PASSES = K // (P * PACK)
+R_PASSES = H // (P * PACK)
 TILES = H // P
 BANK = 512
+BANKS = 8
+E_BANKS = 4
 HALF = M // 2
 W2_PIECE = 256
+W1_WORDS = P * PACK // 2
+W1_SCALE_WORDS = H // 4
+SKEW_RUN = 2 * (PACK - 1) + 1
 
 
 def tile_list_lane_tap_corrections_kernel(
@@ -36,93 +42,66 @@ def tile_list_lane_tap_corrections_kernel(
         ring = ctx.enter_context(tc.tile_pool(name="ring", bufs=2))
         psum = ctx.enter_context(tc.psum_pool(name="psum", bufs=1))
 
-        def bank(j):
-            return psum.tile([P, BANK], F32, name="bank%d" % (j % 8), tag="bank%d" % (j % 8))
+        def bank(number):
+            tag = "bank%d" % (number % BANKS)
+            return psum.tile([P, BANK], F32, name=tag, tag=tag)
 
-        scale_win = keep.tile([P, T], U8, name="scale_win", tag="slot_a", align_bytes=64)
-        nc.gpsimd.memset(scale_win[:].bitcast(I32), 0)
-        offs_t = lists.tile([P, S // 16], U16, name="offs_t")
-        nc.sync.dma_start(offs_t[:], offs)
-        skew_t = keep.tile([P, PASSES2, 8], F32, name="skew_t")
-
-        def load_skew(l):
+        def load_w1(b):
+            raw = keep.tile([P, K_PASSES * W1_WORDS], I32, name="w1_raw%d" % b, align_bytes=64)
             nc.sync.dma_start(
-                skew_t[l:P:2, :, 0:7],
-                skew.rearrange("(b w j) -> w b j", b=PASSES2, j=8)[:, :, l : l + 7],
-            )
-
-        load_skew(0)
-        load_skew(1)
-        for a in range(PASSES1):
-            nc.sync.dma_start(scale_win[a:P:8, :].bitcast(I32), tab_scales[a].bitcast(I32))
-
-        def load_words(a, slot):
-            win = keep.tile([P, T], I32, name="words_win%d" % a, tag=slot, align_bytes=64)
-            nc.sync.dma_start(win[:], tab_words[a].rearrange("p t i -> p (t i)").bitcast(I32))
-            return win
-
-        wins = [load_words(0, "slot_b")]
-        w1s_raw = keep.tile([P, PASSES1 * 256], I32, name="w1s_raw", align_bytes=64)
-        nc.vector.memset(w1s_raw[:], 0)
-        for r in range(4):
-            nc.sync.dma_start(
-                w1s_raw[r:P:32, :].rearrange("d (a c) -> d a c", a=PASSES1),
-                w1_scales[:, r:16:4, :].bitcast(I32).rearrange("a d c -> d a c"),
-            )
-
-        def load_w1(b, slot):
-            raw = keep.tile([P, PASSES1 * 256], I32, name="w1_raw%d" % b, tag=slot, align_bytes=64)
-            nc.sync.dma_start(
-                raw[:].rearrange("p (a c) -> p a c", a=PASSES1),
-                w1_words.bitcast(I32).rearrange("a p c -> p a c")[:, :, 256 * b : 256 * (b + 1)],
+                raw[:].rearrange("p (a c) -> p a c", a=K_PASSES),
+                w1_words.bitcast(I32).rearrange("a p c -> p a c")[:, :, W1_WORDS * b : W1_WORDS * (b + 1)],
             )
             return raw
 
-        w1_raw = [load_w1(0, "slot_d")]
-        wins.append(load_words(1, "slot_c"))
+        skew_runs = keep.tile([P, R_PASSES, 8], F32, name="skew_runs")
+
+        def load_skew(l):
+            nc.sync.dma_start(
+                skew_runs[l:P:2, :, 0:SKEW_RUN],
+                skew.rearrange("(b w j) -> w b j", b=R_PASSES, j=8)[:, :, l : l + SKEW_RUN],
+            )
+
+        def load_words(a, buffer):
+            window = keep.tile([P, T], I32, name="words_window%d" % a, tag=buffer, align_bytes=64)
+            nc.sync.dma_start(window[:], tab_words[a].rearrange("p t i -> p (t i)").bitcast(I32))
+            return window
+
+        scale_window = keep.tile([P, T], U8, name="scale_window", tag="early", align_bytes=64)
+        nc.gpsimd.memset(scale_window[:].bitcast(I32), 0)
+        offs_t = lists.tile([P, S // GROUP], U16, name="offs_t")
+        nc.sync.dma_start(offs_t[:], offs)
+        w1_raw = [load_w1(0)]
+        load_skew(0)
+        for a in range(K_PASSES):
+            nc.sync.dma_start(scale_window[a:P:8, :].bitcast(I32), tab_scales[a].bitcast(I32))
+        windows = [load_words(0, "first")]
+
+        w1_scales_raw = keep.tile([P, K_PASSES * W1_SCALE_WORDS], I32, name="w1_scales_raw", align_bytes=64)
+        nc.vector.memset(w1_scales_raw[:], 0)
+        for s in range(4):
+            nc.sync.dma_start(
+                w1_scales_raw[s:P:32, :].rearrange("d (a c) -> d a c", a=K_PASSES),
+                w1_scales[:, s:16:4, :].bitcast(I32).rearrange("a d c -> d a c"),
+            )
+        load_skew(1)
+        windows.append(load_words(1, "second"))
 
         neg_skew = keep.tile([P, TILES], F32, name="neg_skew")
         nc.scalar.activation(
-            neg_skew[:].rearrange("p (b t) -> p b t", t=PACK), skew_t[:, :, 0:7:2], ACT.Copy, scale=-1.0
+            neg_skew[:].rearrange("p (b t) -> p b t", t=PACK), skew_runs[:, :, 0:SKEW_RUN:2], ACT.Copy, scale=-1.0
         )
 
         v_planes = []
-        for a in range(PASSES1):
+        for a in range(K_PASSES):
             plane = keep.tile([P, S], U8, name="v_plane%d" % a, align_bytes=64)
             nc.vector.memset(plane[:].bitcast(I32), 0)
             v_planes.append(plane)
 
-        scale_got = keep.tile([P, S], U8, name="scale_got", align_bytes=64)
-        nc.vector.tensor_copy(scale_got[:], scale_win[:].indirect(offs_t[:]))
-        for a in range(PASSES1):
-            for r in range(4):
-                nc.sync.dma_start(
-                    v_planes[a][r:P:32, :].bitcast(I32),
-                    scale_got[8 * r + a : P : 32, :].bitcast(I32),
-                )
-                if (a, r) == (1, 1):
-                    wins.append(load_words(2, "slot_a"))
-        w1_raw.append(load_w1(1, "slot_e"))
-        pos2_t = lists.tile([P, M // 16], U16, name="pos2_t")
-        nc.sync.dma_start(pos2_t[:], pos2)
-        pos1_t = lists.tile([P, M // 16], U16, name="pos1_t")
-        nc.sync.dma_start(pos1_t[:], pos1)
-
-        v_words = {}
-
-        def gather_words(a, first, width):
-            got = keep.tile([P, width], U32, name="v_words%d_%d" % (a, first), align_bytes=64)
-            cols = slice(first // 16, (first + width) // 16)
-            nc.vector.tensor_copy(got[:], wins[a][:].bitcast(U32).indirect(offs_t[:, cols]))
-            for j in range(0, width, BANK):
-                v_words[a, (first + j) // BANK] = got[:, j : j + BANK]
-
-        gather_words(0, 0, S)
-
         w1_codes = []
 
         def deal_w1(b):
-            codes = keep.tile([P, PASSES1 * 256], I32, name="w1_codes%d" % b, align_bytes=64)
+            codes = keep.tile([P, K_PASSES * W1_WORDS], I32, name="w1_codes%d" % b, align_bytes=64)
             nc.vector.tensor_copy(
                 codes[:].rearrange("p (a t w i) -> p w a t i", t=PACK, w=16, i=4),
                 w1_raw[b][:].rearrange("p (a w i t) -> p w a t i", t=PACK, w=16, i=4),
@@ -130,96 +109,119 @@ def tile_list_lane_tap_corrections_kernel(
             w1_codes.append(codes)
 
         deal_w1(0)
-        w1_plane = keep.tile([P, PASSES1 * 256], I32, name="w1_plane", align_bytes=64)
+
+        scales_got = keep.tile([P, S], U8, name="scales_got", align_bytes=64)
+        nc.vector.tensor_copy(scales_got[:], scale_window[:].indirect(offs_t[:]))
+        for a in range(K_PASSES):
+            for s in range(4):
+                nc.sync.dma_start(
+                    v_planes[a][s:P:32, :].bitcast(I32),
+                    scales_got[8 * s + a : P : 32, :].bitcast(I32),
+                )
+                if (a, s) == (1, 1):
+                    windows.append(load_words(2, "early"))
+        w1_raw.append(load_w1(1))
+        pos2_t = lists.tile([P, M // GROUP], U16, name="pos2_t")
+        nc.sync.dma_start(pos2_t[:], pos2)
+        pos1_t = lists.tile([P, M // GROUP], U16, name="pos1_t")
+        nc.sync.dma_start(pos1_t[:], pos1)
+
+        v_words = {}
+
+        def gather_words(a, first, width):
+            got = keep.tile([P, width], U32, name="v_words%d_%d" % (a, first), align_bytes=64)
+            entries = offs_t[:, first // GROUP : (first + width) // GROUP]
+            nc.vector.tensor_copy(got[:], windows[a][:].bitcast(U32).indirect(entries))
+            for j in range(0, width, BANK):
+                v_words[a, (first + j) // BANK] = got[:, j : j + BANK]
+
+        gather_words(0, 0, S)
+        w1_plane = keep.tile([P, K_PASSES * W1_SCALE_WORDS], I32, name="w1_plane", align_bytes=64)
         nc.vector.tensor_copy(
             w1_plane[:].bitcast(U16).rearrange("p (g t w i) -> p g w t i", t=PACK, w=8, i=8),
-            w1s_raw[:].bitcast(U16).rearrange("p (g w i t) -> p g w t i", t=PACK, w=8, i=8),
+            w1_scales_raw[:].bitcast(U16).rearrange("p (g w i t) -> p g w t i", t=PACK, w=8, i=8),
         )
-        gather_words(1, 0, BANK)
-        gather_words(1, BANK, BANK)
-        gather_words(2, 0, BANK)
-        gather_words(2, BANK, BANK)
+        for a in range(1, K_PASSES):
+            for half in range(2):
+                gather_words(a, half * BANK, BANK)
 
         w2_raw = []
-        for b in range(PASSES2):
-            raw = keep.tile([P, PACK * N], F32, name="w2_raw%d" % b, tag=("slot_d", "slot_c")[b], align_bytes=64)
+        for b in range(R_PASSES):
+            raw = keep.tile([P, PACK * N], F32, name="w2_raw%d" % b, tag=("first", "second")[b], align_bytes=64)
             for l in range(2):
                 nc.sync.dma_start(
                     raw[l:P:2, :].rearrange("w (t n) -> w t n", t=PACK),
-                    w2.rearrange("(b w t l) n -> b l w t n", b=PASSES2, t=PACK, l=2)[b, l],
+                    w2.rearrange("(b w t l) n -> b l w t n", b=R_PASSES, t=PACK, l=2)[b, l],
                 )
             w2_raw.append(raw)
-        slope_t = keep.tile([P, N // P, M], F32, name="slope_t", tag="slot_b", align_bytes=64)
+        slope_t = keep.tile([P, N // P, M], F32, name="slope_t", tag="early", align_bytes=64)
         nc.sync.dma_start(slope_t[:], slope.rearrange("(c p) m -> p c m", p=P))
 
-        w2_codes = [keep.tile([P, N], U32, name="w2_codes%d" % b, align_bytes=64) for b in range(PASSES2)]
-        w2_plane = [keep.tile([P, N], U8, name="w2_plane%d" % b, align_bytes=64) for b in range(PASSES2)]
-        w2_round = {}
+        def round_and_interleave(rounded, slots):
+            nc.scalar.copy(
+                rounded.rearrange("p (c i t) -> p c t i", i=4, t=PACK),
+                slots.rearrange("p t (c i) -> p c t i", i=4),
+            )
+
+        w2_codes = [keep.tile([P, N], U32, name="w2_codes%d" % b, align_bytes=64) for b in range(R_PASSES)]
+        w2_plane = [keep.tile([P, N], U8, name="w2_plane%d" % b, align_bytes=64) for b in range(R_PASSES)]
+        w2_rounded = {}
 
         def round_w2(piece):
             b, j = divmod(piece, N // W2_PIECE)
-            rounded = ring.tile([P, W2_PIECE * PACK], BF16, name="w2_round", align_bytes=64, bufs=3)
-            src = w2_raw[b][:].rearrange("p (t n) -> p t n", t=PACK)[:, :, j * W2_PIECE : (j + 1) * W2_PIECE]
-            nc.scalar.copy(
-                rounded[:].rearrange("p (c i t) -> p c t i", i=4, t=PACK),
-                src.rearrange("p t (c i) -> p c t i", i=4),
-            )
-            w2_round[piece] = rounded
+            rounded = ring.tile([P, W2_PIECE * PACK], BF16, name="w2_rounded", align_bytes=64, bufs=3)
+            slots = w2_raw[b][:].rearrange("p (t n) -> p t n", t=PACK)
+            round_and_interleave(rounded[:], slots[:, :, j * W2_PIECE : (j + 1) * W2_PIECE])
+            w2_rounded[piece] = rounded
 
         def quantize_w2(piece):
             b, j = divmod(piece, N // W2_PIECE)
             cols = slice(j * W2_PIECE, (j + 1) * W2_PIECE)
-            nc.vector.quantize_mx(w2_codes[b][:, cols].bitcast(FP8X4), w2_plane[b][:, cols], w2_round[piece][:])
+            nc.vector.quantize_mx(w2_codes[b][:, cols].bitcast(FP8X4), w2_plane[b][:, cols], w2_rounded[piece][:])
 
         e_banks = {}
 
-        def first_pass(i, hf, a):
+        def first_pass(i, half, a):
             if a == 0:
-                e_banks[i, hf] = bank((2 * i + hf) % 4)
+                e_banks[i, half] = bank((2 * i + half) % E_BANKS)
             b, t = divmod(i, PACK)
-            codes = w1_codes[b][:, 256 * a + 64 * t : 256 * a + 64 * (t + 1)]
-            scales = w1_plane[:, 256 * a + 32 * i : 256 * a + 32 * (i + 1)]
+            code0 = W1_WORDS * a + P // 2 * t
+            scale0 = W1_SCALE_WORDS * a + P // 4 * i
             nc.tensor.matmul_mx(
-                e_banks[i, hf][:],
-                lhsT=codes.bitcast(FP4X4),
-                lhsT_scale=scales.bitcast(U8),
-                rhs=v_words[a, hf].bitcast(FP8X4),
-                rhs_scale=v_planes[a][:, hf * BANK : (hf + 1) * BANK],
+                e_banks[i, half][:],
+                lhsT=w1_codes[b][:, code0 : code0 + P // 2].bitcast(FP4X4),
+                lhsT_scale=w1_plane[:, scale0 : scale0 + P // 4].bitcast(U8),
+                rhs=v_words[a, half].bitcast(FP8X4),
+                rhs_scale=v_planes[a][:, half * BANK : (half + 1) * BANK],
                 start=(a == 0),
-                stop=(a == PASSES1 - 1),
+                stop=(a == K_PASSES - 1),
             )
-
-        for a in range(PASSES1):
-            for hf in range(2):
-                for i in range(2):
-                    first_pass(i, hf, a)
-
 
         e_abs = {}
 
-        def magnitude(i, hf):
+        def magnitude(i, half):
             mag = ring.tile([P, BANK], F32, name="e_abs", bufs=6)
-            nc.scalar.activation(mag[:], e_banks[i, hf][:], ACT.Abs)
-            e_abs[i, hf] = mag
+            nc.scalar.activation(mag[:], e_banks[i, half][:], ACT.Abs)
+            e_abs[i, half] = mag
 
         h_tiles = [keep.tile([P, S], F32, name="h%d" % i, align_bytes=64) for i in range(TILES)]
-        after = [keep.tile([P, M], F32, name="after%d" % i, align_bytes=64) for i in range(TILES)]
-        spans = [(0, 0, M), (1, 0, HALF), (1, HALF, HALF)]
-        x_f32 = {
-            (b, m0): keep.tile([P, PACK, width], F32, name="x%d_%d" % (b, m0), align_bytes=64)
-            for b, m0, width in spans
-        }
-        x_round, x_codes, x_plane = {}, {}, {}
 
-        def features(i, hf):
+        def features(i, half):
             nc.vector.scalar_tensor_tensor(
-                h_tiles[i][:, hf * BANK : (hf + 1) * BANK],
-                e_abs[i, hf][:],
+                h_tiles[i][:, half * BANK : (half + 1) * BANK],
+                e_abs[i, half][:],
                 neg_skew[:, i : i + 1],
-                e_banks[i, hf][:],
+                e_banks[i, half][:],
                 ALU.mult,
                 ALU.add,
             )
+
+        after = [keep.tile([P, M], F32, name="after%d" % i, align_bytes=64) for i in range(TILES)]
+        x_slots = {
+            (b, m0): keep.tile([P, PACK, width], F32, name="x%d_%d" % (b, m0), align_bytes=64)
+            for b, m0, width in ((0, 0, M), (1, 0, HALF), (1, HALF, HALF))
+        }
+        x_rounded, x_codes, x_plane = {}, {}, {}
 
         def pick_after(i):
             picked = ring.tile([P, M], F32, name="picked", bufs=3)
@@ -229,35 +231,33 @@ def tile_list_lane_tap_corrections_kernel(
         def pick_before(i, m0, width):
             b, t = divmod(i, PACK)
             nc.vector.tensor_tensor(
-                x_f32[b, m0][:, t, :],
-                h_tiles[i][:].indirect(pos1_t[:, m0 // 16 : (m0 + width) // 16]),
+                x_slots[b, m0][:, t, :],
+                h_tiles[i][:].indirect(pos1_t[:, m0 // GROUP : (m0 + width) // GROUP]),
                 after[i][:, m0 : m0 + width],
                 ALU.add,
             )
 
         def round_x(b, m0, width):
-            rounded = keep.tile([P, width * PACK], BF16, name="x_round%d_%d" % (b, m0), align_bytes=64)
+            rounded = keep.tile([P, width * PACK], BF16, name="x_rounded%d_%d" % (b, m0), align_bytes=64)
             for j in range(0, width, HALF):
-                nc.scalar.copy(
-                    rounded[:, j * PACK : (j + HALF) * PACK].rearrange("p (c i t) -> p c t i", i=4, t=PACK),
-                    x_f32[b, m0][:, :, j : j + HALF].rearrange("p t (c i) -> p c t i", i=4),
-                )
-            x_round[b, m0] = rounded
+                round_and_interleave(rounded[:, j * PACK : (j + HALF) * PACK], x_slots[b, m0][:, :, j : j + HALF])
+            x_rounded[b, m0] = rounded
 
         def quantize_x(b, m0, width):
             codes = keep.tile([P, width], U32, name="x_codes%d_%d" % (b, m0), align_bytes=64)
             plane = keep.tile([P, width], U8, name="x_plane%d_%d" % (b, m0), align_bytes=64)
-            nc.vector.quantize_mx(codes[:].bitcast(FP8X4), plane[:], x_round[b, m0][:])
+            nc.vector.quantize_mx(codes[:].bitcast(FP8X4), plane[:], x_rounded[b, m0][:])
             for j in range(0, width, HALF):
                 x_codes[b, (m0 + j) // HALF] = codes[:, j : j + HALF]
                 x_plane[b, (m0 + j) // HALF] = plane[:, j : j + HALF]
 
         y_banks = {}
+        pairs = N // P // 2
 
         def second_pass(b, part):
-            for pair in range(N // P // 2):
+            for pair in range(pairs):
                 if b == 0:
-                    y_banks[part, pair] = bank(4 + 3 * part + pair)
+                    y_banks[part, pair] = bank(E_BANKS + pairs * part + pair)
                 for u in range(2):
                     c = 2 * pair + u
                     nc.tensor.matmul_mx(
@@ -267,33 +267,38 @@ def tile_list_lane_tap_corrections_kernel(
                         rhs=x_codes[b, part].bitcast(FP8X4),
                         rhs_scale=x_plane[b, part],
                         start=(b == 0 and u == 0),
-                        stop=(b == PASSES2 - 1 and u == 1),
+                        stop=(b == R_PASSES - 1 and u == 1),
                     )
 
         def finish(part, c0, count):
             cols = slice(part * HALF, (part + 1) * HALF)
             pair, u = divmod(c0, 2)
-            res = keep.tile([P, count, HALF], F32, name="res%d_%d" % (part, c0))
+            result = keep.tile([P, count, HALF], F32, name="result%d_%d" % (part, c0))
             nc.vector.tensor_tensor(
-                res[:],
+                result[:],
                 y_banks[part, pair][:].rearrange("p (u m) -> p u m", u=2)[:, u : u + count, :],
                 slope_t[:, c0 : c0 + count, cols],
                 ALU.mult,
             )
-            nc.sync.dma_start(out.rearrange("(c p) m -> p c m", p=P)[:, c0 : c0 + count, cols], res[:])
+            nc.sync.dma_start(out.rearrange("(c p) m -> p c m", p=P)[:, c0 : c0 + count, cols], result[:])
 
-        for hf in range(2):
+        for a in range(K_PASSES):
+            for half in range(2):
+                for i in range(2):
+                    first_pass(i, half, a)
+        for half in range(2):
             for i in range(2):
-                magnitude(i, hf)
+                magnitude(i, half)
         features(0, 0)
         features(1, 0)
         features(0, 1)
+
         for i in range(TILES):
             if i + 2 < TILES:
-                for hf in range(2):
-                    for a in range(PASSES1):
-                        first_pass(i + 2, hf, a)
-                    magnitude(i + 2, hf)
+                for half in range(2):
+                    for a in range(K_PASSES):
+                        first_pass(i + 2, half, a)
+                    magnitude(i + 2, half)
             pick_after(i)
             if i >= 2:
                 round_w2(i - 2)
@@ -301,7 +306,7 @@ def tile_list_lane_tap_corrections_kernel(
                 if i >= 1:
                     features(i + 1, 0)
                 features(i + 1, 1)
-            if i == 1:
+            if i + 3 == PACK:
                 deal_w1(1)
             if i >= 3:
                 quantize_w2(i - 3)
@@ -310,7 +315,8 @@ def tile_list_lane_tap_corrections_kernel(
                 round_x(0, 0, M)
             if i == PACK + 1:
                 quantize_x(0, 0, M)
-        quantize_w2(5)
+        quantize_w2(TILES - 3)
+
         second_pass(0, 0)
         second_pass(0, 1)
         round_x(1, 0, HALF)

from contextlib import ExitStack

import concourse.mybir as mybir

K, T, S, H, M, N = 1536, 2048, 1024, 1024, 512, 768
FLOPS = 2 * K * H * S + 2 * H * N * M

F32 = mybir.dt.float32
BF16 = mybir.dt.bfloat16
I32 = mybir.dt.int32
U32 = mybir.dt.uint32
U16 = mybir.dt.uint16
U8 = mybir.dt.uint8
FP8X4 = mybir.dt.float8_e4m3fn_x4
FP4X4 = mybir.dt.float4_e2m1fn_x4
ALU = mybir.AluOpType
ACT = mybir.ActivationFunctionType

P = 128
PACK = 4
GROUP = 16
K_PASSES = K // (P * PACK)
R_PASSES = H // (P * PACK)
TILES = H // P
BANK = 512
BANKS = 8
E_BANKS = 4
HALF = M // 2
W2_PIECE = 256
W1_WORDS = P * PACK // 2
W1_SCALE_WORDS = H // 4
SKEW_RUN = 2 * (PACK - 1) + 1


def tile_list_lane_tap_corrections_kernel(
    tc, tab_words, tab_scales, offs, w1_words, w1_scales, skew, pos1, pos2, w2, slope, out
):
    nc = tc.nc
    with ExitStack() as ctx:
        lists = ctx.enter_context(tc.tile_pool(name="lists", bufs=1))
        keep = ctx.enter_context(tc.tile_pool(name="keep", bufs=1))
        ring = ctx.enter_context(tc.tile_pool(name="ring", bufs=2))
        psum = ctx.enter_context(tc.psum_pool(name="psum", bufs=1))

        def bank(number):
            tag = "bank%d" % (number % BANKS)
            return psum.tile([P, BANK], F32, name=tag, tag=tag)

        def load_w1(b):
            raw = keep.tile([P, K_PASSES * W1_WORDS], I32, name="w1_raw%d" % b, align_bytes=64)
            nc.sync.dma_start(
                raw[:].rearrange("p (a c) -> p a c", a=K_PASSES),
                w1_words.bitcast(I32).rearrange("a p c -> p a c")[:, :, W1_WORDS * b : W1_WORDS * (b + 1)],
            )
            return raw

        skew_runs = keep.tile([P, R_PASSES, 8], F32, name="skew_runs")

        def load_skew(l):
            nc.sync.dma_start(
                skew_runs[l:P:2, :, 0:SKEW_RUN],
                skew.rearrange("(b w j) -> w b j", b=R_PASSES, j=8)[:, :, l : l + SKEW_RUN],
            )

        def load_words(a, buffer):
            window = keep.tile([P, T], I32, name="words_window%d" % a, tag=buffer, align_bytes=64)
            nc.sync.dma_start(window[:], tab_words[a].rearrange("p t i -> p (t i)").bitcast(I32))
            return window

        scale_window = keep.tile([P, T], U8, name="scale_window", tag="early", align_bytes=64)
        nc.gpsimd.memset(scale_window[:].bitcast(I32), 0)
        offs_t = lists.tile([P, S // GROUP], U16, name="offs_t")
        nc.sync.dma_start(offs_t[:], offs)
        w1_raw = [load_w1(0)]
        load_skew(0)
        for a in range(K_PASSES):
            nc.sync.dma_start(scale_window[a:P:8, :].bitcast(I32), tab_scales[a].bitcast(I32))
        windows = [load_words(0, "first")]

        w1_scales_raw = keep.tile([P, K_PASSES * W1_SCALE_WORDS], I32, name="w1_scales_raw", align_bytes=64)
        nc.vector.memset(w1_scales_raw[:], 0)
        for s in range(4):
            nc.sync.dma_start(
                w1_scales_raw[s:P:32, :].rearrange("d (a c) -> d a c", a=K_PASSES),
                w1_scales[:, s:16:4, :].bitcast(I32).rearrange("a d c -> d a c"),
            )
        load_skew(1)
        windows.append(load_words(1, "second"))

        neg_skew = keep.tile([P, TILES], F32, name="neg_skew")
        nc.scalar.activation(
            neg_skew[:].rearrange("p (b t) -> p b t", t=PACK), skew_runs[:, :, 0:SKEW_RUN:2], ACT.Copy, scale=-1.0
        )

        v_planes = []
        for a in range(K_PASSES):
            plane = keep.tile([P, S], U8, name="v_plane%d" % a, align_bytes=64)
            nc.vector.memset(plane[:].bitcast(I32), 0)
            v_planes.append(plane)

        w1_codes = []

        def deal_w1(b):
            codes = keep.tile([P, K_PASSES * W1_WORDS], I32, name="w1_codes%d" % b, align_bytes=64)
            nc.vector.tensor_copy(
                codes[:].rearrange("p (a t w i) -> p w a t i", t=PACK, w=16, i=4),
                w1_raw[b][:].rearrange("p (a w i t) -> p w a t i", t=PACK, w=16, i=4),
            )
            w1_codes.append(codes)

        deal_w1(0)

        scales_got = keep.tile([P, S], U8, name="scales_got", align_bytes=64)
        nc.vector.tensor_copy(scales_got[:], scale_window[:].indirect(offs_t[:]))
        for a in range(K_PASSES):
            for s in range(4):
                nc.sync.dma_start(
                    v_planes[a][s:P:32, :].bitcast(I32),
                    scales_got[8 * s + a : P : 32, :].bitcast(I32),
                )
                if (a, s) == (1, 1):
                    windows.append(load_words(2, "early"))
        w1_raw.append(load_w1(1))
        pos2_t = lists.tile([P, M // GROUP], U16, name="pos2_t")
        nc.sync.dma_start(pos2_t[:], pos2)
        pos1_t = lists.tile([P, M // GROUP], U16, name="pos1_t")
        nc.sync.dma_start(pos1_t[:], pos1)

        v_words = {}

        def gather_words(a, first, width):
            got = keep.tile([P, width], U32, name="v_words%d_%d" % (a, first), align_bytes=64)
            entries = offs_t[:, first // GROUP : (first + width) // GROUP]
            nc.vector.tensor_copy(got[:], windows[a][:].bitcast(U32).indirect(entries))
            for j in range(0, width, BANK):
                v_words[a, (first + j) // BANK] = got[:, j : j + BANK]

        gather_words(0, 0, S)
        w1_plane = keep.tile([P, K_PASSES * W1_SCALE_WORDS], I32, name="w1_plane", align_bytes=64)
        nc.vector.tensor_copy(
            w1_plane[:].bitcast(U16).rearrange("p (g t w i) -> p g w t i", t=PACK, w=8, i=8),
            w1_scales_raw[:].bitcast(U16).rearrange("p (g w i t) -> p g w t i", t=PACK, w=8, i=8),
        )
        for a in range(1, K_PASSES):
            for half in range(2):
                gather_words(a, half * BANK, BANK)

        w2_raw = []
        for b in range(R_PASSES):
            raw = keep.tile([P, PACK * N], F32, name="w2_raw%d" % b, tag=("first", "second")[b], align_bytes=64)
            for l in range(2):
                nc.sync.dma_start(
                    raw[l:P:2, :].rearrange("w (t n) -> w t n", t=PACK),
                    w2.rearrange("(b w t l) n -> b l w t n", b=R_PASSES, t=PACK, l=2)[b, l],
                )
            w2_raw.append(raw)
        slope_t = keep.tile([P, N // P, M], F32, name="slope_t", tag="early", align_bytes=64)
        nc.sync.dma_start(slope_t[:], slope.rearrange("(c p) m -> p c m", p=P))

        def round_and_interleave(rounded, slots):
            nc.scalar.copy(
                rounded.rearrange("p (c i t) -> p c t i", i=4, t=PACK),
                slots.rearrange("p t (c i) -> p c t i", i=4),
            )

        w2_codes = [keep.tile([P, N], U32, name="w2_codes%d" % b, align_bytes=64) for b in range(R_PASSES)]
        w2_plane = [keep.tile([P, N], U8, name="w2_plane%d" % b, align_bytes=64) for b in range(R_PASSES)]
        w2_rounded = {}

        def round_w2(piece):
            b, j = divmod(piece, N // W2_PIECE)
            rounded = ring.tile([P, W2_PIECE * PACK], BF16, name="w2_rounded", align_bytes=64, bufs=3)
            slots = w2_raw[b][:].rearrange("p (t n) -> p t n", t=PACK)
            round_and_interleave(rounded[:], slots[:, :, j * W2_PIECE : (j + 1) * W2_PIECE])
            w2_rounded[piece] = rounded

        def quantize_w2(piece):
            b, j = divmod(piece, N // W2_PIECE)
            cols = slice(j * W2_PIECE, (j + 1) * W2_PIECE)
            nc.vector.quantize_mx(w2_codes[b][:, cols].bitcast(FP8X4), w2_plane[b][:, cols], w2_rounded[piece][:])

        e_banks = {}

        def first_pass(i, half, a):
            if a == 0:
                e_banks[i, half] = bank((2 * i + half) % E_BANKS)
            b, t = divmod(i, PACK)
            code0 = W1_WORDS * a + P // 2 * t
            scale0 = W1_SCALE_WORDS * a + P // 4 * i
            nc.tensor.matmul_mx(
                e_banks[i, half][:],
                lhsT=w1_codes[b][:, code0 : code0 + P // 2].bitcast(FP4X4),
                lhsT_scale=w1_plane[:, scale0 : scale0 + P // 4].bitcast(U8),
                rhs=v_words[a, half].bitcast(FP8X4),
                rhs_scale=v_planes[a][:, half * BANK : (half + 1) * BANK],
                start=(a == 0),
                stop=(a == K_PASSES - 1),
            )

        e_abs = {}

        def magnitude(i, half):
            mag = ring.tile([P, BANK], F32, name="e_abs", bufs=6)
            nc.scalar.activation(mag[:], e_banks[i, half][:], ACT.Abs)
            e_abs[i, half] = mag

        h_tiles = [keep.tile([P, S], F32, name="h%d" % i, align_bytes=64) for i in range(TILES)]

        def features(i, half):
            nc.vector.scalar_tensor_tensor(
                h_tiles[i][:, half * BANK : (half + 1) * BANK],
                e_abs[i, half][:],
                neg_skew[:, i : i + 1],
                e_banks[i, half][:],
                ALU.mult,
                ALU.add,
            )

        after = [keep.tile([P, M], F32, name="after%d" % i, align_bytes=64) for i in range(TILES)]
        x_slots = {
            (b, m0): keep.tile([P, PACK, width], F32, name="x%d_%d" % (b, m0), align_bytes=64)
            for b, m0, width in ((0, 0, M), (1, 0, HALF), (1, HALF, HALF))
        }
        x_rounded, x_codes, x_plane = {}, {}, {}

        def pick_after(i):
            picked = ring.tile([P, M], F32, name="picked", bufs=3)
            nc.vector.tensor_copy(picked[:], h_tiles[i][:].indirect(pos2_t[:]))
            nc.scalar.activation(after[i][:], picked[:], ACT.Abs)

        def pick_before(i, m0, width):
            b, t = divmod(i, PACK)
            nc.vector.tensor_tensor(
                x_slots[b, m0][:, t, :],
                h_tiles[i][:].indirect(pos1_t[:, m0 // GROUP : (m0 + width) // GROUP]),
                after[i][:, m0 : m0 + width],
                ALU.add,
            )

        def round_x(b, m0, width):
            rounded = keep.tile([P, width * PACK], BF16, name="x_rounded%d_%d" % (b, m0), align_bytes=64)
            for j in range(0, width, HALF):
                round_and_interleave(rounded[:, j * PACK : (j + HALF) * PACK], x_slots[b, m0][:, :, j : j + HALF])
            x_rounded[b, m0] = rounded

        def quantize_x(b, m0, width):
            codes = keep.tile([P, width], U32, name="x_codes%d_%d" % (b, m0), align_bytes=64)
            plane = keep.tile([P, width], U8, name="x_plane%d_%d" % (b, m0), align_bytes=64)
            nc.vector.quantize_mx(codes[:].bitcast(FP8X4), plane[:], x_rounded[b, m0][:])
            for j in range(0, width, HALF):
                x_codes[b, (m0 + j) // HALF] = codes[:, j : j + HALF]
                x_plane[b, (m0 + j) // HALF] = plane[:, j : j + HALF]

        y_banks = {}
        pairs = N // P // 2

        def second_pass(b, part):
            for pair in range(pairs):
                if b == 0:
                    y_banks[part, pair] = bank(E_BANKS + pairs * part + pair)
                for u in range(2):
                    c = 2 * pair + u
                    nc.tensor.matmul_mx(
                        y_banks[part, pair][:, u * HALF : (u + 1) * HALF],
                        lhsT=w2_codes[b][:, c * P : (c + 1) * P].bitcast(FP8X4),
                        lhsT_scale=w2_plane[b][:, c * P : (c + 1) * P],
                        rhs=x_codes[b, part].bitcast(FP8X4),
                        rhs_scale=x_plane[b, part],
                        start=(b == 0 and u == 0),
                        stop=(b == R_PASSES - 1 and u == 1),
                    )

        def finish(part, c0, count):
            cols = slice(part * HALF, (part + 1) * HALF)
            pair, u = divmod(c0, 2)
            result = keep.tile([P, count, HALF], F32, name="result%d_%d" % (part, c0))
            nc.vector.tensor_tensor(
                result[:],
                y_banks[part, pair][:].rearrange("p (u m) -> p u m", u=2)[:, u : u + count, :],
                slope_t[:, c0 : c0 + count, cols],
                ALU.mult,
            )
            nc.sync.dma_start(out.rearrange("(c p) m -> p c m", p=P)[:, c0 : c0 + count, cols], result[:])

        for a in range(K_PASSES):
            for half in range(2):
                for i in range(2):
                    first_pass(i, half, a)
        for half in range(2):
            for i in range(2):
                magnitude(i, half)
        features(0, 0)
        features(1, 0)
        features(0, 1)

        for i in range(TILES):
            if i + 2 < TILES:
                for half in range(2):
                    for a in range(K_PASSES):
                        first_pass(i + 2, half, a)
                    magnitude(i + 2, half)
            pick_after(i)
            if i >= 2:
                round_w2(i - 2)
            if i + 1 < TILES:
                if i >= 1:
                    features(i + 1, 0)
                features(i + 1, 1)
            if i + 3 == PACK:
                deal_w1(1)
            if i >= 3:
                quantize_w2(i - 3)
            pick_before(i, 0, M if i < PACK else HALF)
            if i == PACK - 1:
                round_x(0, 0, M)
            if i == PACK + 1:
                quantize_x(0, 0, M)
        quantize_w2(TILES - 3)

        second_pass(0, 0)
        second_pass(0, 1)
        round_x(1, 0, HALF)
        for i in range(PACK, TILES - 1):
            pick_before(i, HALF, HALF)
        quantize_x(1, 0, HALF)
        second_pass(1, 0)
        pick_before(TILES - 1, HALF, HALF)
        round_x(1, HALF, HALF)
        finish(0, 0, 2)
        finish(0, 2, 2)
        quantize_x(1, HALF, HALF)
        second_pass(1, 1)
        finish(0, 4, 2)
        finish(1, 0, 2)
        finish(1, 2, 2)
        finish(1, 4, 1)
        finish(1, 5, 1)
